import numpy as np
import ml_dtypes


def mxq(x, axis, fmt="e4m3"):
    dtype, down = {"e4m3": (ml_dtypes.float8_e4m3fn, 7), "e5m2": (ml_dtypes.float8_e5m2, 14)}[fmt]
    v = np.moveaxis(np.asarray(x, np.float32).astype(ml_dtypes.bfloat16).astype(np.float64), axis, -1)
    blocks = v.reshape(v.shape[:-1] + (-1, 32))
    amax = np.abs(blocks).max(-1, keepdims=True)
    byte = np.maximum(np.where(amax > 0, np.frexp(amax)[1] - 1 + 127, 0) - down, 1)
    scale = np.exp2(byte - 127.0)
    codes = (blocks / scale).astype(np.float32).astype(dtype).astype(np.float64)
    return np.moveaxis((codes * scale).reshape(v.shape), -1, axis)


WIDE = False


def mx_kscale(k):
    if not WIDE:
        return np.ones(k)
    levels = np.array([10, -10, 5, -5, 0])
    if k % 512:
        return np.exp2(np.random.permutation(np.resize(levels, k // 32))).repeat(32)
    a = np.empty((k // 512, 16))
    for p in range(k // 512):
        a[p, :8] = np.random.permutation(np.resize(levels, 8))
        for g in range(8):
            far = levels[np.abs(levels - a[p, g]) >= 10]
            a[p, g + 8] = far[np.random.randint(len(far))]
    return np.exp2(a.ravel()).repeat(32)


def f64(x):
    return np.asarray(x).astype(np.float64)


def striped(idx):
    return np.tile(idx.reshape(-1, 16).T, (8, 1)).astype(np.uint16)


def unstriped(offs):
    return offs[:16].T.reshape(-1).astype(np.int64)


E2M1 = np.array([0.0, 0.5, 1.0, 1.5, 2.0, 3.0, 4.0, 6.0, -0.0, -0.5, -1.0, -1.5, -2.0, -3.0, -4.0, -6.0])


def pack_weight(w, fmt):
    k, n = w.shape
    w = f64(np.asarray(w, np.float32).astype(ml_dtypes.bfloat16)).reshape(k // 32, 32, n)
    amax = np.abs(w).max(1)
    if fmt == "e4m3":
        byte = np.frexp(amax)[1] - 1 + 127 - 7
    else:
        mant, ex = np.frexp(amax / 6.0)
        byte = np.where(mant > 0.5, ex, ex - 1) + 127
    byte = np.clip(np.where(amax > 0, byte, 1), 1, 254)
    scaled = (w * np.exp2(127.0 - byte)[:, None, :]).reshape(k, n).astype(np.float32)
    by_word = np.ascontiguousarray(scaled.reshape(k // 512, 128, 4, n).transpose(0, 1, 3, 2))
    if fmt == "e4m3":
        words = by_word.astype(ml_dtypes.float8_e4m3fn).view(np.uint8)
    else:
        c = by_word.astype(ml_dtypes.float4_e2m1fn).view(np.uint8) & 0xF
        words = (c[..., 0::2] | (c[..., 1::2] << 4)).reshape(k // 512, 128, 2 * n)
    return np.ascontiguousarray(words), np.ascontiguousarray(byte.astype(np.uint8).reshape(k // 512, 16, n))


def unpack_weight(words, scales, fmt):
    g, _, n = scales.shape
    words = np.ascontiguousarray(words).reshape(g, 128, n, -1)
    if fmt == "e4m3":
        vals = words.view(ml_dtypes.float8_e4m3fn).astype(np.float64)
    else:
        nib = np.empty((g, 128, n, 4), np.uint8)
        nib[..., 0::2] = words & 0xF
        nib[..., 1::2] = words >> 4
        vals = E2M1[nib]
    vals = vals * np.repeat(np.exp2(scales.astype(np.float64) - 127.0), 8, axis=1)[..., None]
    return vals.transpose(0, 1, 3, 2).reshape(g * 512, n)


def gelu(v):
    return 0.5 * v * (1.0 + np.tanh(np.sqrt(2.0 / np.pi) * (v + 0.044715 * v**3)))


K, H, T, S, T3, S2, P = 512, 1024, 4096, 1024, 2048, 1024, 512

def setup_inputs():
    n = np.random.standard_normal
    s = mx_kscale(K)[:, None]
    u = mx_kscale(H)[:, None]
    tab_words, tab_scales = pack_weight(n((K, T)) * s, "e4m3")
    tab2_words, tab2_scales = pack_weight(n((H, T3)) / np.sqrt(H) / u, "e4m3")
    w4_words, w4_scales = pack_weight(1.3 * n((K, H)) / np.sqrt(K) / s, "e2m1")
    return {
        "tab_words": tab_words, "tab_scales": tab_scales,
        "offs": striped(np.random.permutation(T)[:S]),
        "tab2_words": tab2_words, "tab2_scales": tab2_scales,
        "offs2": striped(np.random.permutation(T3)[:S2]),
        "pos1": striped(np.random.permutation(S)[:P]),
        "pos2": striped(np.random.permutation(S)[:P]),
        "wa": (0.52 * n((K, H)) / np.sqrt(K) / s).astype(np.float32),
        "w4_words": w4_words, "w4_scales": w4_scales,
        "gain": (1.5 * np.exp(0.4 * n(H)) * u[:, 0]).astype(np.float32),
        "main": np.exp(0.5 * n(H)).astype(np.float32),
        "stock": np.exp(0.4 * n(S2)).astype(np.float32),
    }

def reference(tab_words, tab_scales, offs, tab2_words, tab2_scales, offs2, pos1, pos2,
              wa, w4_words, w4_scales, gain, main, stock):
    v = unpack_weight(tab_words, tab_scales, "e4m3")[:, unstriped(offs)]
    v2 = unpack_weight(tab2_words, tab2_scales, "e4m3")[:, unstriped(offs2)]
    w4 = unpack_weight(w4_words, w4_scales, "e2m1")
    wave = np.cos(mxq(f64(wa), 0, "e4m3").T @ v)
    body = np.tanh(w4.T @ v)
    h = f64(gain)[:, None] * (wave * body)
    x1 = mxq(h[:, unstriped(pos1)], 0, "e4m3")
    x2 = mxq(f64(main)[:, None] * h[:, unstriped(pos2)], 0, "e4m3")
    e1 = v2.T @ x1
    e2 = v2.T @ x2
    return f64(stock)[:, None] * np.maximum(e1, e2)

@@ -1,0 +1,265 @@
+import math
+from contextlib import ExitStack
+
+import concourse.mybir as mybir
+
+K, H, T, S, T3, S2, MENUS = 512, 1024, 4096, 1024, 2048, 1024, 512
+FLOPS = 2 * (2 * K * H * S + 2 * H * S2 * MENUS)
+
+F32 = mybir.dt.float32
+BF16 = mybir.dt.bfloat16
+I32 = mybir.dt.int32
+U32 = mybir.dt.uint32
+U16 = mybir.dt.uint16
+U8 = mybir.dt.uint8
+FP8X4 = mybir.dt.float8_e4m3fn_x4
+FP4X4 = mybir.dt.float4_e2m1fn_x4
+ACT = mybir.ActivationFunctionType
+ALU = mybir.AluOpType
+
+P = 128
+PACK = 4
+BANK = 512
+PER_COL = 16
+R_PASSES = H // (P * PACK)
+R_TILES = H // P
+M_TILES = S2 // P
+TWO_PI = 2.0 * math.pi
+TURN_OFFSET = 31.25
+TILES_COUNTED_ON_VECTOR = 2
+EARLY_M_TILES = 3
+EARLY_BOTTLES = 768
+AT_W4_RAW = 0
+AT_TAB_PLANE = S + 4 * T3 + 2 * S
+AT_WA_RAW = AT_TAB_PLANE + 2 * S
+AT_W4_PLANE_RAW = AT_WA_RAW + 4 * PACK * BANK
+AT_TAB = AT_W4_PLANE_RAW + 128 + T3
+
+
+def tile_list_wine_course_pairing_kernel(
+    tc, tab_words, tab_scales, offs, tab2_words, tab2_scales, offs2, pos1, pos2,
+    wa, w4_words, w4_scales, gain, main, stock, out,
+):
+    nc = tc.nc
+    with ExitStack() as ctx:
+        keep = ctx.enter_context(tc.tile_pool(name="keep", bufs=1))
+        reuse = ctx.enter_context(tc.tile_pool(name="reuse", bufs=1))
+        work = ctx.enter_context(tc.tile_pool(name="work", bufs=2))
+        psum = ctx.enter_context(tc.psum_pool(name="psum", bufs=1))
+
+        def bank(index):
+            return psum.tile([P, BANK], F32, name="bank%d" % index, tag="bank%d" % index)
+
+        def placed(shape, dtype, name, offset):
+            return reuse.tile(shape, dtype, name=name, offset=offset, align_bytes=64)
+
+        def load_list(src, entries, name):
+            tile = keep.tile([P, entries // PER_COL], U16, name=name)
+            nc.sync.dma_start(tile[:], src)
+            return tile
+
+        def gather(dst, window, offsets, first, last):
+            nc.vector.tensor_copy(
+                dst[:, first:last], window.indirect(offsets[:, first // PER_COL : last // PER_COL])
+            )
+
+        dishes = load_list(offs, S, "dishes")
+        bottles = load_list(offs2, S2, "bottles")
+        starters = load_list(pos1, MENUS, "starters")
+        mains = load_list(pos2, MENUS, "mains")
+        tab_sb = placed([P, T], I32, "tab_sb", AT_TAB)
+        nc.sync.dma_start(tab_sb[:], tab_words[0].rearrange("p t i -> p (t i)").bitcast(I32))
+        w4_raw = placed([P, 2 * H], U8, "w4_raw", AT_W4_RAW)
+        nc.scalar.dma_start(w4_raw[:].bitcast(I32), w4_words[0].bitcast(I32))
+
+        tab_plane = placed([P, T], U8, "tab_plane", AT_TAB_PLANE)
+        w4_plane_raw = placed([P, H], U8, "w4_plane_raw", AT_W4_PLANE_RAW)
+        nc.vector.memset(tab_plane[:].bitcast(I32), 0)
+        nc.vector.memset(w4_plane_raw[:].bitcast(I32), 0)
+        for q in range(4):
+            nc.scalar.dma_start(
+                tab_plane[32 * q : 32 * q + 4, :].bitcast(I32), tab_scales[0, 4 * q : 4 * q + 4, :].bitcast(I32)
+            )
+        for q in range(4):
+            nc.scalar.dma_start(
+                w4_plane_raw[32 * q : 32 * q + 4, :].bitcast(I32), w4_scales[0, 4 * q : 4 * q + 4, :].bitcast(I32)
+            )
+
+        def load_tab2(a, offset):
+            words = placed([P, T3], I32, "tab2_sb%d" % a, offset)
+            nc.sync.dma_start(words[:], tab2_words[a].rearrange("p t i -> p (t i)").bitcast(I32))
+            return words
+
+        def load_wa(a):
+            raw = placed([P, PACK, BANK], F32, "wa_raw%d" % a, AT_WA_RAW)
+            nc.sync.dma_start(raw[:], wa[:, a * BANK : (a + 1) * BANK].rearrange("(p j) c -> p j c", j=PACK))
+            return raw
+
+        one = keep.tile([P, 1], F32)
+        nc.vector.memset(one[:], 1.0)
+        sin_bias = keep.tile([P, 1], F32)
+        nc.vector.tensor_scalar(sin_bias[:], one[:], TWO_PI * TURN_OFFSET, None, ALU.mult)
+
+        w4_codes = keep.tile([P, 2 * H], U8, align_bytes=64)
+        nc.vector.tensor_copy(
+            w4_codes[:].bitcast(U16).rearrange("p (a t m) -> p a t m", a=R_PASSES, t=PACK),
+            w4_raw[:].bitcast(U16).rearrange("p (a m t) -> p a t m", a=R_PASSES, t=PACK),
+        )
+        v_codes = placed([P, S], U32, "v_codes", AT_TAB_PLANE - 2 * S)
+        v_plane = placed([P, S], U8, "v_plane", AT_W4_RAW)
+        gather(v_plane, tab_plane[:], dishes, 0, S)
+        gather(v_codes, tab_sb[:].bitcast(U32), dishes, 0, BANK)
+        w4_plane = keep.tile([P, H], U8, align_bytes=64)
+        nc.vector.tensor_copy(
+            w4_plane[:].rearrange("p (a t m) -> p a t m", a=R_PASSES, t=PACK),
+            w4_plane_raw[:].rearrange("p (a m t) -> p a t m", a=R_PASSES, t=PACK),
+        )
+        gather(v_codes, tab_sb[:].bitcast(U32), dishes, BANK, S)
+
+        def first_stage(acc, codes, plane, half):
+            cols = slice(half * BANK, (half + 1) * BANK)
+            nc.tensor.matmul_mx(
+                out=acc[:], lhsT=codes, lhsT_scale=plane,
+                rhs=v_codes[:, cols].bitcast(FP8X4), rhs_scale=v_plane[:, cols],
+                start=True, stop=True,
+            )
+
+        body = [keep.tile([P, S], F32, name="body%d" % i) for i in range(R_TILES)]
+        for half in range(2):
+            for i in range(R_TILES):
+                acc = bank(4 + i % 4)
+                first_stage(
+                    acc, w4_codes[:, 2 * P * i : 2 * P * (i + 1)].bitcast(FP4X4), w4_plane[:, P * i : P * (i + 1)], half
+                )
+                nc.scalar.activation(body[i][:, half * BANK : (half + 1) * BANK], acc[:], ACT.Tanh)
+
+        tab2_sb = [load_tab2(0, AT_W4_RAW + S)]
+        wa_first = load_wa(0)
+        gain_sb = placed([P, R_PASSES, PACK], F32, "gain_sb", AT_W4_PLANE_RAW)
+        nc.sync.dma_start(gain_sb[:], gain.rearrange("(a p t) -> p a t", a=R_PASSES, t=PACK))
+        main_sb = placed([P, R_PASSES, PACK], F32, "main_sb", AT_W4_PLANE_RAW + 64)
+        nc.sync.dma_start(main_sb[:], main.rearrange("(a p t) -> p a t", a=R_PASSES, t=PACK))
+        tab2_plane = placed([P, T3], U8, "tab2_plane", AT_W4_PLANE_RAW + 128)
+        nc.vector.memset(tab2_plane[:].bitcast(I32), 0)
+        for q in range(4):
+            nc.sync.dma_start(
+                tab2_plane[32 * q : 32 * q + 8, :].bitcast(I32), tab2_scales[:, 4 * q : 4 * q + 4, :].bitcast(I32)
+            )
+        tab2_sb.append(load_tab2(1, AT_TAB))
+        v2_codes = [keep.tile([P, S2], U32, name="v2_codes%d" % a, align_bytes=64) for a in range(R_PASSES)]
+        v2_plane = keep.tile([P, S2], U8, align_bytes=64)
+
+        wa_codes = keep.tile([P, H], U32, align_bytes=64)
+        wa_plane = keep.tile([P, H], U8, align_bytes=64)
+
+        def quantise_wa(a, raw):
+            woven = work.tile([P, PACK * BANK], BF16, name="wa_woven", align_bytes=64)
+            nc.vector.tensor_copy(
+                woven[:].rearrange("p (t m j) -> p m t j", t=PACK, j=PACK),
+                raw[:].rearrange("p j (m t) -> p m t j", t=PACK),
+            )
+            cols = slice(a * BANK, (a + 1) * BANK)
+            nc.vector.quantize_mx(out=wa_codes[:, cols].bitcast(FP8X4), scales=wa_plane[:, cols], in_=woven[:])
+
+        def wave_of(i):
+            turns = work.tile([P, S], F32, name="turns")
+            for half in range(2):
+                acc = bank((2 * i + half) % 4 if i < 4 else half)
+                first_stage(acc, wa_codes[:, P * i : P * (i + 1)].bitcast(FP8X4), wa_plane[:, P * i : P * (i + 1)], half)
+                whole = work.tile([P, BANK], U32, name="whole", bufs=3)
+                if i < TILES_COUNTED_ON_VECTOR:
+                    nc.vector.tensor_scalar(
+                        whole[:].bitcast(I32), acc[:], 1.0 / TWO_PI, TURN_OFFSET, ALU.mult, ALU.add
+                    )
+                else:
+                    nc.scalar.activation(whole[:], acc[:], ACT.Copy, bias=TURN_OFFSET, scale=1.0 / TWO_PI)
+                nc.vector.scalar_tensor_tensor(
+                    turns[:, half * BANK : (half + 1) * BANK], acc[:], 1.0 / TWO_PI, whole[:].bitcast(I32),
+                    ALU.mult, ALU.subtract,
+                )
+            wave = work.tile([P, S], F32, name="wave", bufs=3)
+            nc.scalar.activation(wave[:], turns[:], ACT.Sin, bias=sin_bias[:], scale=TWO_PI)
+            return wave
+
+        gather(v2_codes[0], tab2_sb[0][:].bitcast(U32), bottles, 0, EARLY_BOTTLES)
+        quantise_wa(0, wa_first)
+        waves = {0: wave_of(0)}
+        gather(v2_plane, tab2_plane[:], bottles, 0, EARLY_BOTTLES)
+        gather(v2_codes[1], tab2_sb[1][:].bitcast(U32), bottles, 0, EARLY_BOTTLES)
+        quantise_wa(1, load_wa(1))
+        stock_sb = placed([P, M_TILES], F32, "stock_sb", AT_WA_RAW)
+        with nc.allow_non_contiguous_dma(reason="one stock value a partition"):
+            nc.sync.dma_start(stock_sb[:], stock.rearrange("(i p) -> p i", p=P))
+
+        x_codes = [[keep.tile([P, MENUS], U32, name="x_codes%d%d" % (c, a), align_bytes=64) for a in range(R_PASSES)] for c in range(2)]
+        x_plane = [[keep.tile([P, MENUS], U8, name="x_plane%d%d" % (c, a), align_bytes=64) for a in range(R_PASSES)] for c in range(2)]
+        picked = [[keep.tile([P, PACK, MENUS], BF16, name="picked%d%d" % (c, a)) for a in range(R_PASSES)] for c in range(2)]
+        x_woven = [[keep.tile([P, PACK * MENUS], BF16, name="x_woven%d%d" % (c, a), align_bytes=64) for a in range(R_PASSES)] for c in range(2)]
+
+        def weave(copy, c, a, first, last):
+            copy(
+                x_woven[c][a][:, PACK * first : PACK * last].rearrange("p (n i t) -> p n t i", i=4, t=PACK),
+                picked[c][a][:, :, first:last].rearrange("p t (n i) -> p n t i", i=4),
+            )
+
+        def quantise_x(c, a):
+            nc.vector.quantize_mx(out=x_codes[c][a][:].bitcast(FP8X4), scales=x_plane[c][a][:], in_=x_woven[c][a][:])
+
+        def second_stage(acc, m, c, a, start, stop):
+            cols = slice(m * P, (m + 1) * P)
+            nc.tensor.matmul_mx(
+                out=acc[:], lhsT=v2_codes[a][:, cols].bitcast(FP8X4), lhsT_scale=v2_plane[4 * a : P, cols],
+                rhs=x_codes[c][a][:].bitcast(FP8X4), rhs_scale=x_plane[c][a][:],
+                start=start, stop=stop,
+            )
+
+        def score_banks(m):
+            pair = (m + 1) % 4
+            return [bank(2 * pair), bank(2 * pair + 1)]
+
+        early = {}
+        for i in range(R_TILES):
+            a, t = divmod(i, PACK)
+            h = work.tile([P, S], F32, name="h")
+            nc.vector.scalar_tensor_tensor(h[:], waves[i][:], gain_sb[:, a, t : t + 1], body[i][:], ALU.mult, ALU.mult)
+            if i + 1 < R_TILES:
+                waves[i + 1] = wave_of(i + 1)
+            for_mains = work.tile([P, MENUS], F32, name="for_mains")
+            nc.vector.tensor_copy(for_mains[:], h[:].indirect(mains[:]))
+            nc.vector.tensor_copy(picked[0][a][:, t, :], h[:].indirect(starters[:]))
+            nc.scalar.activation(picked[1][a][:, t, :], for_mains[:], ACT.Copy, scale=main_sb[:, a, t : t + 1])
+            if a == 1:
+                c, part = divmod(t, 2)
+                weave(nc.scalar.copy, c, 0, part * MENUS // 2, (part + 1) * MENUS // 2)
+                if part == 1:
+                    quantise_x(c, 0)
+                    for m in range(EARLY_M_TILES):
+                        if c == 0:
+                            early[m] = score_banks(m)
+                        second_stage(early[m][c], m, c, 0, True, False)
+
+        weave(nc.vector.tensor_copy, 0, 1, 0, MENUS)
+        weave(nc.scalar.copy, 1, 1, 0, MENUS)
+        quantise_x(0, 1)
+        quantise_x(1, 1)
+        gather(v2_plane, tab2_plane[:], bottles, EARLY_BOTTLES, S2)
+        for a in range(R_PASSES):
+            gather(v2_codes[a], tab2_sb[a][:].bitcast(U32), bottles, EARLY_BOTTLES, S2)
+
+        for m in range(M_TILES):
+            if m < EARLY_M_TILES:
+                scores = early[m]
+                for c in range(2):
+                    second_stage(scores[c], m, c, 1, False, True)
+            else:
+                scores = score_banks(m)
+                for c in range(2):
+                    second_stage(scores[c], m, c, 1, True, False)
+                    second_stage(scores[c], m, c, 0, False, True)
+            starter_score = work.tile([P, MENUS], F32, name="starter_score", bufs=3)
+            nc.scalar.copy(starter_score[:], scores[0][:])
+            larger = work.tile([P, MENUS], F32, name="larger", bufs=3)
+            nc.vector.tensor_tensor(larger[:], scores[1][:], starter_score[:], ALU.max)
+            result = work.tile([P, MENUS], F32, name="result", bufs=4)
+            nc.scalar.activation(result[:], larger[:], ACT.Copy, scale=stock_sb[:, m : m + 1])
+            nc.sync.dma_start(out[m * P : (m + 1) * P, :], result[:])

@@ -20,20 +20,27 @@ ALU = mybir.AluOpType
 P = 128
 PACK = 4
 BANK = 512
+QUADRANTS = 4
 PER_COL = 16
 R_PASSES = H // (P * PACK)
 R_TILES = H // P
 M_TILES = S2 // P
+BANK_PAIRS = 4
+
 TWO_PI = 2.0 * math.pi
 TURN_OFFSET = 31.25
-TILES_COUNTED_ON_VECTOR = 2
-EARLY_M_TILES = 3
-EARLY_BOTTLES = 768
+
+EARLY_M_TILES = BANK_PAIRS
+
 AT_W4_RAW = 0
-AT_TAB_PLANE = S + 4 * T3 + 2 * S
-AT_WA_RAW = AT_TAB_PLANE + 2 * S
+AT_TAB2_FIRST = AT_W4_RAW + S
+AT_V_CODES = AT_TAB2_FIRST + 4 * T3
+AT_TAB_PLANE = AT_V_CODES + 2 * S
+AT_WA_RAW = AT_V_CODES + 4 * S
 AT_W4_PLANE_RAW = AT_WA_RAW + 4 * PACK * BANK
-AT_TAB = AT_W4_PLANE_RAW + 128 + T3
+AT_MAIN = AT_W4_PLANE_RAW + 64
+AT_TAB2_PLANE = AT_MAIN + 64
+AT_TAB = AT_TAB2_PLANE + T3
 
 
 def tile_list_wine_course_pairing_kernel(
@@ -47,8 +54,9 @@ def tile_list_wine_course_pairing_kernel(
         work = ctx.enter_context(tc.tile_pool(name="work", bufs=2))
         psum = ctx.enter_context(tc.psum_pool(name="psum", bufs=1))
 
-        def bank(index):
-            return psum.tile([P, BANK], F32, name="bank%d" % index, tag="bank%d" % index)
+        def bank(pair, side):
+            name = "bank%d" % (2 * pair + side)
+            return psum.tile([P, BANK], F32, name=name, tag=name)
 
         def placed(shape, dtype, name, offset):
             return reuse.tile(shape, dtype, name=name, offset=offset, align_bytes=64)
@@ -58,10 +66,7 @@ def tile_list_wine_course_pairing_kernel(
             nc.sync.dma_start(tile[:], src)
             return tile
 
-        def gather(dst, window, offsets, first, last):
-            nc.vector.tensor_copy(
-                dst[:, first:last], window.indirect(offsets[:, first // PER_COL : last // PER_COL])
-            )
+        halves = [(half, slice(half * BANK, (half + 1) * BANK)) for half in range(2)]
 
         dishes = load_list(offs, S, "dishes")
         bottles = load_list(offs2, S2, "bottles")
@@ -76,24 +81,12 @@ def tile_list_wine_course_pairing_kernel(
         w4_plane_raw = placed([P, H], U8, "w4_plane_raw", AT_W4_PLANE_RAW)
         nc.vector.memset(tab_plane[:].bitcast(I32), 0)
         nc.vector.memset(w4_plane_raw[:].bitcast(I32), 0)
-        for q in range(4):
-            nc.scalar.dma_start(
-                tab_plane[32 * q : 32 * q + 4, :].bitcast(I32), tab_scales[0, 4 * q : 4 * q + 4, :].bitcast(I32)
-            )
-        for q in range(4):
-            nc.scalar.dma_start(
-                w4_plane_raw[32 * q : 32 * q + 4, :].bitcast(I32), w4_scales[0, 4 * q : 4 * q + 4, :].bitcast(I32)
-            )
-
-        def load_tab2(a, offset):
-            words = placed([P, T3], I32, "tab2_sb%d" % a, offset)
-            nc.sync.dma_start(words[:], tab2_words[a].rearrange("p t i -> p (t i)").bitcast(I32))
-            return words
-
-        def load_wa(a):
-            raw = placed([P, PACK, BANK], F32, "wa_raw%d" % a, AT_WA_RAW)
-            nc.sync.dma_start(raw[:], wa[:, a * BANK : (a + 1) * BANK].rearrange("(p j) c -> p j c", j=PACK))
-            return raw
+        for plane, scales in ((tab_plane, tab_scales), (w4_plane_raw, w4_scales)):
+            for quad in range(QUADRANTS):
+                nc.scalar.dma_start(
+                    plane[32 * quad : 32 * quad + 4, :].bitcast(I32),
+                    scales[0, 4 * quad : 4 * quad + 4, :].bitcast(I32),
+                )
 
         one = keep.tile([P, 1], F32)
         nc.vector.memset(one[:], 1.0)
@@ -105,19 +98,24 @@ def tile_list_wine_course_pairing_kernel(
             w4_codes[:].bitcast(U16).rearrange("p (a t m) -> p a t m", a=R_PASSES, t=PACK),
             w4_raw[:].bitcast(U16).rearrange("p (a m t) -> p a t m", a=R_PASSES, t=PACK),
         )
-        v_codes = placed([P, S], U32, "v_codes", AT_TAB_PLANE - 2 * S)
+
+        v_codes = placed([P, S], U32, "v_codes", AT_V_CODES)
         v_plane = placed([P, S], U8, "v_plane", AT_W4_RAW)
-        gather(v_plane, tab_plane[:], dishes, 0, S)
-        gather(v_codes, tab_sb[:].bitcast(U32), dishes, 0, BANK)
+        nc.vector.tensor_copy(v_plane[:], tab_plane[:].indirect(dishes[:]))
+
+        def gather_dishes(cols):
+            offsets = dishes[:, cols.start // PER_COL : cols.stop // PER_COL]
+            nc.vector.tensor_copy(v_codes[:, cols], tab_sb[:].bitcast(U32).indirect(offsets))
+
+        gather_dishes(halves[0][1])
         w4_plane = keep.tile([P, H], U8, align_bytes=64)
         nc.vector.tensor_copy(
             w4_plane[:].rearrange("p (a t m) -> p a t m", a=R_PASSES, t=PACK),
             w4_plane_raw[:].rearrange("p (a m t) -> p a t m", a=R_PASSES, t=PACK),
         )
-        gather(v_codes, tab_sb[:].bitcast(U32), dishes, BANK, S)
+        gather_dishes(halves[1][1])
 
-        def first_stage(acc, codes, plane, half):
-            cols = slice(half * BANK, (half + 1) * BANK)
+        def first_stage(acc, codes, plane, cols):
             nc.tensor.matmul_mx(
                 out=acc[:], lhsT=codes, lhsT_scale=plane,
                 rhs=v_codes[:, cols].bitcast(FP8X4), rhs_scale=v_plane[:, cols],
@@ -125,76 +123,105 @@ def tile_list_wine_course_pairing_kernel(
             )
 
         body = [keep.tile([P, S], F32, name="body%d" % i) for i in range(R_TILES)]
-        for half in range(2):
+        for half, cols in halves:
             for i in range(R_TILES):
-                acc = bank(4 + i % 4)
-                first_stage(
-                    acc, w4_codes[:, 2 * P * i : 2 * P * (i + 1)].bitcast(FP4X4), w4_plane[:, P * i : P * (i + 1)], half
-                )
-                nc.scalar.activation(body[i][:, half * BANK : (half + 1) * BANK], acc[:], ACT.Tanh)
+                acc = bank(2 + i % 4 // 2, i % 2)
+                codes = w4_codes[:, 2 * P * i : 2 * P * (i + 1)].bitcast(FP4X4)
+                first_stage(acc, codes, w4_plane[:, P * i : P * (i + 1)], cols)
+                nc.scalar.activation(body[i][:, cols], acc[:], ACT.Tanh)
 
-        tab2_sb = [load_tab2(0, AT_W4_RAW + S)]
+        def load_tab2(a, offset):
+            words = placed([P, T3], I32, "tab2_sb%d" % a, offset)
+            nc.sync.dma_start(words[:], tab2_words[a].rearrange("p t i -> p (t i)").bitcast(I32))
+            return words
+
+        def load_wa(a):
+            raw = placed([P, PACK, BANK], F32, "wa_raw%d" % a, AT_WA_RAW)
+            nc.sync.dma_start(raw[:], wa[:, a * BANK : (a + 1) * BANK].rearrange("(p j) c -> p j c", j=PACK))
+            return raw
+
+        tab2_sb = [load_tab2(0, AT_TAB2_FIRST)]
         wa_first = load_wa(0)
         gain_sb = placed([P, R_PASSES, PACK], F32, "gain_sb", AT_W4_PLANE_RAW)
         nc.sync.dma_start(gain_sb[:], gain.rearrange("(a p t) -> p a t", a=R_PASSES, t=PACK))
-        main_sb = placed([P, R_PASSES, PACK], F32, "main_sb", AT_W4_PLANE_RAW + 64)
+        main_sb = placed([P, R_PASSES, PACK], F32, "main_sb", AT_MAIN)
         nc.sync.dma_start(main_sb[:], main.rearrange("(a p t) -> p a t", a=R_PASSES, t=PACK))
-        tab2_plane = placed([P, T3], U8, "tab2_plane", AT_W4_PLANE_RAW + 128)
-        nc.vector.memset(tab2_plane[:].bitcast(I32), 0)
-        for q in range(4):
+        tab2_plane = placed([P, T3], U8, "tab2_plane", AT_TAB2_PLANE)
+        nc.gpsimd.memset(tab2_plane[:].bitcast(I32), 0)
+        for quad in range(QUADRANTS):
             nc.sync.dma_start(
-                tab2_plane[32 * q : 32 * q + 8, :].bitcast(I32), tab2_scales[:, 4 * q : 4 * q + 4, :].bitcast(I32)
+                tab2_plane[32 * quad : 32 * quad + 4 * R_PASSES, :].bitcast(I32),
+                tab2_scales[:, 4 * quad : 4 * quad + 4, :].bitcast(I32),
             )
         tab2_sb.append(load_tab2(1, AT_TAB))
-        v2_codes = [keep.tile([P, S2], U32, name="v2_codes%d" % a, align_bytes=64) for a in range(R_PASSES)]
-        v2_plane = keep.tile([P, S2], U8, align_bytes=64)
 
         wa_codes = keep.tile([P, H], U32, align_bytes=64)
         wa_plane = keep.tile([P, H], U8, align_bytes=64)
 
-        def quantise_wa(a, raw):
+        def quantise_wa(a, raw, copy):
             woven = work.tile([P, PACK * BANK], BF16, name="wa_woven", align_bytes=64)
-            nc.vector.tensor_copy(
+            copy(
                 woven[:].rearrange("p (t m j) -> p m t j", t=PACK, j=PACK),
                 raw[:].rearrange("p j (m t) -> p m t j", t=PACK),
             )
             cols = slice(a * BANK, (a + 1) * BANK)
             nc.vector.quantize_mx(out=wa_codes[:, cols].bitcast(FP8X4), scales=wa_plane[:, cols], in_=woven[:])
 
-        def wave_of(i):
+        def cosine(i):
+            rows = slice(P * i, P * (i + 1))
             turns = work.tile([P, S], F32, name="turns")
-            for half in range(2):
-                acc = bank((2 * i + half) % 4 if i < 4 else half)
-                first_stage(acc, wa_codes[:, P * i : P * (i + 1)].bitcast(FP8X4), wa_plane[:, P * i : P * (i + 1)], half)
-                whole = work.tile([P, BANK], U32, name="whole", bufs=3)
-                if i < TILES_COUNTED_ON_VECTOR:
+            for half, cols in halves:
+                acc = bank(i % 2 if i < PACK else 0, half)
+                first_stage(acc, wa_codes[:, rows].bitcast(FP8X4), wa_plane[:, rows], cols)
+                count = work.tile([P, BANK], U32, name="count", bufs=3)
+                if i == 0:
                     nc.vector.tensor_scalar(
-                        whole[:].bitcast(I32), acc[:], 1.0 / TWO_PI, TURN_OFFSET, ALU.mult, ALU.add
+                        count[:].bitcast(I32), acc[:], 1.0 / TWO_PI, TURN_OFFSET, ALU.mult, ALU.add
                     )
                 else:
-                    nc.scalar.activation(whole[:], acc[:], ACT.Copy, bias=TURN_OFFSET, scale=1.0 / TWO_PI)
+                    nc.scalar.activation(count[:], acc[:], ACT.Copy, bias=TURN_OFFSET, scale=1.0 / TWO_PI)
                 nc.vector.scalar_tensor_tensor(
-                    turns[:, half * BANK : (half + 1) * BANK], acc[:], 1.0 / TWO_PI, whole[:].bitcast(I32),
-                    ALU.mult, ALU.subtract,
+                    turns[:, cols], acc[:], 1.0 / TWO_PI, count[:].bitcast(I32), ALU.mult, ALU.subtract
                 )
             wave = work.tile([P, S], F32, name="wave", bufs=3)
             nc.scalar.activation(wave[:], turns[:], ACT.Sin, bias=sin_bias[:], scale=TWO_PI)
             return wave
 
-        gather(v2_codes[0], tab2_sb[0][:].bitcast(U32), bottles, 0, EARLY_BOTTLES)
-        quantise_wa(0, wa_first)
-        waves = {0: wave_of(0)}
-        gather(v2_plane, tab2_plane[:], bottles, 0, EARLY_BOTTLES)
-        gather(v2_codes[1], tab2_sb[1][:].bitcast(U32), bottles, 0, EARLY_BOTTLES)
-        quantise_wa(1, load_wa(1))
+        def features(i):
+            a, t = divmod(i, PACK)
+            h = work.tile([P, S], F32, name="h", bufs=3)
+            nc.vector.scalar_tensor_tensor(h[:], waves[i][:], gain_sb[:, a, t : t + 1], body[i][:], ALU.mult, ALU.mult)
+            return h
+
+        v2_codes = [keep.tile([P, S2], U32, name="v2_codes%d" % a, align_bytes=64) for a in range(R_PASSES)]
+        v2_plane = keep.tile([P, S2], U8, align_bytes=64)
+        nc.vector.tensor_copy(v2_codes[0][:], tab2_sb[0][:].bitcast(U32).indirect(bottles[:]))
+        quantise_wa(0, wa_first, nc.vector.tensor_copy)
+        waves = {0: cosine(0)}
+        nc.vector.tensor_copy(v2_plane[:], tab2_plane[:].indirect(bottles[:]))
+        nc.vector.tensor_copy(v2_codes[1][:], tab2_sb[1][:].bitcast(U32).indirect(bottles[:]))
+        waves[1] = cosine(1)
+        wa_second = load_wa(1)
         stock_sb = placed([P, M_TILES], F32, "stock_sb", AT_WA_RAW)
         with nc.allow_non_contiguous_dma(reason="one stock value a partition"):
-            nc.sync.dma_start(stock_sb[:], stock.rearrange("(i p) -> p i", p=P))
+            nc.sync.dma_start(stock_sb[:], stock.rearrange("(m p) -> p m", p=P))
 
-        x_codes = [[keep.tile([P, MENUS], U32, name="x_codes%d%d" % (c, a), align_bytes=64) for a in range(R_PASSES)] for c in range(2)]
-        x_plane = [[keep.tile([P, MENUS], U8, name="x_plane%d%d" % (c, a), align_bytes=64) for a in range(R_PASSES)] for c in range(2)]
-        picked = [[keep.tile([P, PACK, MENUS], BF16, name="picked%d%d" % (c, a)) for a in range(R_PASSES)] for c in range(2)]
-        x_woven = [[keep.tile([P, PACK * MENUS], BF16, name="x_woven%d%d" % (c, a), align_bytes=64) for a in range(R_PASSES)] for c in range(2)]
+        picked = [
+            [keep.tile([P, PACK, MENUS], BF16, name="picked%d%d" % (c, a)) for a in range(R_PASSES)]
+            for c in range(2)
+        ]
+        x_woven = [
+            [keep.tile([P, PACK * MENUS], BF16, name="x_woven%d%d" % (c, a), align_bytes=64) for a in range(R_PASSES)]
+            for c in range(2)
+        ]
+        x_codes, x_plane = {}, {}
+
+        def pick(i):
+            a, t = divmod(i, PACK)
+            for_mains = work.tile([P, MENUS], F32, name="for_mains")
+            nc.vector.tensor_copy(for_mains[:], hs[i][:].indirect(mains[:]))
+            nc.vector.tensor_copy(picked[0][a][:, t, :], hs[i][:].indirect(starters[:]))
+            nc.scalar.activation(picked[1][a][:, t, :], for_mains[:], ACT.Copy, scale=main_sb[:, a, t : t + 1])
 
         def weave(copy, c, a, first, last):
             copy(
@@ -203,48 +230,46 @@ def tile_list_wine_course_pairing_kernel(
             )
 
         def quantise_x(c, a):
-            nc.vector.quantize_mx(out=x_codes[c][a][:].bitcast(FP8X4), scales=x_plane[c][a][:], in_=x_woven[c][a][:])
+            x_codes[c, a] = keep.tile([P, MENUS], U32, name="x_codes%d%d" % (c, a), align_bytes=64)
+            x_plane[c, a] = keep.tile([P, MENUS], U8, name="x_plane%d%d" % (c, a), align_bytes=64)
+            nc.vector.quantize_mx(out=x_codes[c, a][:].bitcast(FP8X4), scales=x_plane[c, a][:], in_=x_woven[c][a][:])
 
         def second_stage(acc, m, c, a, start, stop):
             cols = slice(m * P, (m + 1) * P)
             nc.tensor.matmul_mx(
                 out=acc[:], lhsT=v2_codes[a][:, cols].bitcast(FP8X4), lhsT_scale=v2_plane[4 * a : P, cols],
-                rhs=x_codes[c][a][:].bitcast(FP8X4), rhs_scale=x_plane[c][a][:],
+                rhs=x_codes[c, a][:].bitcast(FP8X4), rhs_scale=x_plane[c, a][:],
                 start=start, stop=stop,
             )
 
         def score_banks(m):
-            pair = (m + 1) % 4
-            return [bank(2 * pair), bank(2 * pair + 1)]
+            return [bank((m + 1) % BANK_PAIRS, c) for c in range(2)]
 
         early = {}
+        hs = {0: features(0)}
         for i in range(R_TILES):
-            a, t = divmod(i, PACK)
-            h = work.tile([P, S], F32, name="h")
-            nc.vector.scalar_tensor_tensor(h[:], waves[i][:], gain_sb[:, a, t : t + 1], body[i][:], ALU.mult, ALU.mult)
+            if i == 0:
+                quantise_wa(1, wa_second, nc.scalar.copy)
+            if i + 2 < R_TILES:
+                waves[i + 2] = cosine(i + 2)
             if i + 1 < R_TILES:
-                waves[i + 1] = wave_of(i + 1)
-            for_mains = work.tile([P, MENUS], F32, name="for_mains")
-            nc.vector.tensor_copy(for_mains[:], h[:].indirect(mains[:]))
-            nc.vector.tensor_copy(picked[0][a][:, t, :], h[:].indirect(starters[:]))
-            nc.scalar.activation(picked[1][a][:, t, :], for_mains[:], ACT.Copy, scale=main_sb[:, a, t : t + 1])
-            if a == 1:
-                c, part = divmod(t, 2)
-                weave(nc.scalar.copy, c, 0, part * MENUS // 2, (part + 1) * MENUS // 2)
-                if part == 1:
+                hs[i + 1] = features(i + 1)
+            if i == R_TILES - 1:
+                for c in range(2):
                     quantise_x(c, 0)
                     for m in range(EARLY_M_TILES):
                         if c == 0:
                             early[m] = score_banks(m)
                         second_stage(early[m][c], m, c, 0, True, False)
+            pick(i)
+            if PACK - 1 <= i < R_TILES - 1:
+                c, part = divmod(i - PACK + 1, 2)
+                weave(nc.scalar.copy, c, 0, part * MENUS // 2, (part + 1) * MENUS // 2)
 
         weave(nc.vector.tensor_copy, 0, 1, 0, MENUS)
         weave(nc.scalar.copy, 1, 1, 0, MENUS)
         quantise_x(0, 1)
         quantise_x(1, 1)
-        gather(v2_plane, tab2_plane[:], bottles, EARLY_BOTTLES, S2)
-        for a in range(R_PASSES):
-            gather(v2_codes[a], tab2_sb[a][:].bitcast(U32), bottles, EARLY_BOTTLES, S2)
 
         for m in range(M_TILES):
             if m < EARLY_M_TILES:
@@ -261,5 +286,11 @@ def tile_list_wine_course_pairing_kernel(
             larger = work.tile([P, MENUS], F32, name="larger", bufs=3)
             nc.vector.tensor_tensor(larger[:], scores[1][:], starter_score[:], ALU.max)
             result = work.tile([P, MENUS], F32, name="result", bufs=4)
-            nc.scalar.activation(result[:], larger[:], ACT.Copy, scale=stock_sb[:, m : m + 1])
+            factor = stock_sb[:, m : m + 1]
+            if m == M_TILES - 1:
+                nc.vector.tensor_scalar(result[:], larger[:], factor, None, ALU.mult)
+            elif m % 2 == 0:
+                nc.gpsimd.tensor_scalar(result[:], larger[:], factor, 0.0, ALU.mult, ALU.add)
+            else:
+                nc.scalar.activation(result[:], larger[:], ACT.Copy, scale=factor)
             nc.sync.dma_start(out[m * P : (m + 1) * P, :], result[:])

import math
from contextlib import ExitStack

import concourse.mybir as mybir

K, H, T, S, T3, S2, MENUS = 512, 1024, 4096, 1024, 2048, 1024, 512
FLOPS = 2 * (2 * K * H * S + 2 * H * S2 * MENUS)

F32 = mybir.dt.float32
BF16 = mybir.dt.bfloat16
I32 = mybir.dt.int32
U32 = mybir.dt.uint32
U16 = mybir.dt.uint16
U8 = mybir.dt.uint8
FP8X4 = mybir.dt.float8_e4m3fn_x4
FP4X4 = mybir.dt.float4_e2m1fn_x4
ACT = mybir.ActivationFunctionType
ALU = mybir.AluOpType

P = 128
PACK = 4
BANK = 512
QUADRANTS = 4
PER_COL = 16
R_PASSES = H // (P * PACK)
R_TILES = H // P
M_TILES = S2 // P
BANK_PAIRS = 4

TWO_PI = 2.0 * math.pi
TURN_OFFSET = 31.25

EARLY_M_TILES = BANK_PAIRS

AT_W4_RAW = 0
AT_TAB2_FIRST = AT_W4_RAW + S
AT_V_CODES = AT_TAB2_FIRST + 4 * T3
AT_TAB_PLANE = AT_V_CODES + 2 * S
AT_WA_RAW = AT_V_CODES + 4 * S
AT_W4_PLANE_RAW = AT_WA_RAW + 4 * PACK * BANK
AT_MAIN = AT_W4_PLANE_RAW + 64
AT_TAB2_PLANE = AT_MAIN + 64
AT_TAB = AT_TAB2_PLANE + T3


def tile_list_wine_course_pairing_kernel(
    tc, tab_words, tab_scales, offs, tab2_words, tab2_scales, offs2, pos1, pos2,
    wa, w4_words, w4_scales, gain, main, stock, out,
):
    nc = tc.nc
    with ExitStack() as ctx:
        keep = ctx.enter_context(tc.tile_pool(name="keep", bufs=1))
        reuse = ctx.enter_context(tc.tile_pool(name="reuse", bufs=1))
        work = ctx.enter_context(tc.tile_pool(name="work", bufs=2))
        psum = ctx.enter_context(tc.psum_pool(name="psum", bufs=1))

        def bank(pair, side):
            name = "bank%d" % (2 * pair + side)
            return psum.tile([P, BANK], F32, name=name, tag=name)

        def placed(shape, dtype, name, offset):
            return reuse.tile(shape, dtype, name=name, offset=offset, align_bytes=64)

        def load_list(src, entries, name):
            tile = keep.tile([P, entries // PER_COL], U16, name=name)
            nc.sync.dma_start(tile[:], src)
            return tile

        halves = [(half, slice(half * BANK, (half + 1) * BANK)) for half in range(2)]

        dishes = load_list(offs, S, "dishes")
        bottles = load_list(offs2, S2, "bottles")
        starters = load_list(pos1, MENUS, "starters")
        mains = load_list(pos2, MENUS, "mains")
        tab_sb = placed([P, T], I32, "tab_sb", AT_TAB)
        nc.sync.dma_start(tab_sb[:], tab_words[0].rearrange("p t i -> p (t i)").bitcast(I32))
        w4_raw = placed([P, 2 * H], U8, "w4_raw", AT_W4_RAW)
        nc.scalar.dma_start(w4_raw[:].bitcast(I32), w4_words[0].bitcast(I32))

        tab_plane = placed([P, T], U8, "tab_plane", AT_TAB_PLANE)
        w4_plane_raw = placed([P, H], U8, "w4_plane_raw", AT_W4_PLANE_RAW)
        nc.vector.memset(tab_plane[:].bitcast(I32), 0)
        nc.vector.memset(w4_plane_raw[:].bitcast(I32), 0)
        for plane, scales in ((tab_plane, tab_scales), (w4_plane_raw, w4_scales)):
            for quad in range(QUADRANTS):
                nc.scalar.dma_start(
                    plane[32 * quad : 32 * quad + 4, :].bitcast(I32),
                    scales[0, 4 * quad : 4 * quad + 4, :].bitcast(I32),
                )

        one = keep.tile([P, 1], F32)
        nc.vector.memset(one[:], 1.0)
        sin_bias = keep.tile([P, 1], F32)
        nc.vector.tensor_scalar(sin_bias[:], one[:], TWO_PI * TURN_OFFSET, None, ALU.mult)

        w4_codes = keep.tile([P, 2 * H], U8, align_bytes=64)
        nc.vector.tensor_copy(
            w4_codes[:].bitcast(U16).rearrange("p (a t m) -> p a t m", a=R_PASSES, t=PACK),
            w4_raw[:].bitcast(U16).rearrange("p (a m t) -> p a t m", a=R_PASSES, t=PACK),
        )

        v_codes = placed([P, S], U32, "v_codes", AT_V_CODES)
        v_plane = placed([P, S], U8, "v_plane", AT_W4_RAW)
        nc.vector.tensor_copy(v_plane[:], tab_plane[:].indirect(dishes[:]))

        def gather_dishes(cols):
            offsets = dishes[:, cols.start // PER_COL : cols.stop // PER_COL]
            nc.vector.tensor_copy(v_codes[:, cols], tab_sb[:].bitcast(U32).indirect(offsets))

        gather_dishes(halves[0][1])
        w4_plane = keep.tile([P, H], U8, align_bytes=64)
        nc.vector.tensor_copy(
            w4_plane[:].rearrange("p (a t m) -> p a t m", a=R_PASSES, t=PACK),
            w4_plane_raw[:].rearrange("p (a m t) -> p a t m", a=R_PASSES, t=PACK),
        )
        gather_dishes(halves[1][1])

        def first_stage(acc, codes, plane, cols):
            nc.tensor.matmul_mx(
                out=acc[:], lhsT=codes, lhsT_scale=plane,
                rhs=v_codes[:, cols].bitcast(FP8X4), rhs_scale=v_plane[:, cols],
                start=True, stop=True,
            )

        body = [keep.tile([P, S], F32, name="body%d" % i) for i in range(R_TILES)]
        for half, cols in halves:
            for i in range(R_TILES):
                acc = bank(2 + i % 4 // 2, i % 2)
                codes = w4_codes[:, 2 * P * i : 2 * P * (i + 1)].bitcast(FP4X4)
                first_stage(acc, codes, w4_plane[:, P * i : P * (i + 1)], cols)
                nc.scalar.activation(body[i][:, cols], acc[:], ACT.Tanh)

        def load_tab2(a, offset):
            words = placed([P, T3], I32, "tab2_sb%d" % a, offset)
            nc.sync.dma_start(words[:], tab2_words[a].rearrange("p t i -> p (t i)").bitcast(I32))
            return words

        def load_wa(a):
            raw = placed([P, PACK, BANK], F32, "wa_raw%d" % a, AT_WA_RAW)
            nc.sync.dma_start(raw[:], wa[:, a * BANK : (a + 1) * BANK].rearrange("(p j) c -> p j c", j=PACK))
            return raw

        tab2_sb = [load_tab2(0, AT_TAB2_FIRST)]
        wa_first = load_wa(0)
        gain_sb = placed([P, R_PASSES, PACK], F32, "gain_sb", AT_W4_PLANE_RAW)
        nc.sync.dma_start(gain_sb[:], gain.rearrange("(a p t) -> p a t", a=R_PASSES, t=PACK))
        main_sb = placed([P, R_PASSES, PACK], F32, "main_sb", AT_MAIN)
        nc.sync.dma_start(main_sb[:], main.rearrange("(a p t) -> p a t", a=R_PASSES, t=PACK))
        tab2_plane = placed([P, T3], U8, "tab2_plane", AT_TAB2_PLANE)
        nc.gpsimd.memset(tab2_plane[:].bitcast(I32), 0)
        for quad in range(QUADRANTS):
            nc.sync.dma_start(
                tab2_plane[32 * quad : 32 * quad + 4 * R_PASSES, :].bitcast(I32),
                tab2_scales[:, 4 * quad : 4 * quad + 4, :].bitcast(I32),
            )
        tab2_sb.append(load_tab2(1, AT_TAB))

        wa_codes = keep.tile([P, H], U32, align_bytes=64)
        wa_plane = keep.tile([P, H], U8, align_bytes=64)

        def quantise_wa(a, raw, copy):
            woven = work.tile([P, PACK * BANK], BF16, name="wa_woven", align_bytes=64)
            copy(
                woven[:].rearrange("p (t m j) -> p m t j", t=PACK, j=PACK),
                raw[:].rearrange("p j (m t) -> p m t j", t=PACK),
            )
            cols = slice(a * BANK, (a + 1) * BANK)
            nc.vector.quantize_mx(out=wa_codes[:, cols].bitcast(FP8X4), scales=wa_plane[:, cols], in_=woven[:])

        def cosine(i):
            rows = slice(P * i, P * (i + 1))
            turns = work.tile([P, S], F32, name="turns")
            for half, cols in halves:
                acc = bank(i % 2 if i < PACK else 0, half)
                first_stage(acc, wa_codes[:, rows].bitcast(FP8X4), wa_plane[:, rows], cols)
                count = work.tile([P, BANK], U32, name="count", bufs=3)
                if i == 0:
                    nc.vector.tensor_scalar(
                        count[:].bitcast(I32), acc[:], 1.0 / TWO_PI, TURN_OFFSET, ALU.mult, ALU.add
                    )
                else:
                    nc.scalar.activation(count[:], acc[:], ACT.Copy, bias=TURN_OFFSET, scale=1.0 / TWO_PI)
                nc.vector.scalar_tensor_tensor(
                    turns[:, cols], acc[:], 1.0 / TWO_PI, count[:].bitcast(I32), ALU.mult, ALU.subtract
                )
            wave = work.tile([P, S], F32, name="wave", bufs=3)
            nc.scalar.activation(wave[:], turns[:], ACT.Sin, bias=sin_bias[:], scale=TWO_PI)
            return wave

        def features(i):
            a, t = divmod(i, PACK)
            h = work.tile([P, S], F32, name="h", bufs=3)
            nc.vector.scalar_tensor_tensor(h[:], waves[i][:], gain_sb[:, a, t : t + 1], body[i][:], ALU.mult, ALU.mult)
            return h

        v2_codes = [keep.tile([P, S2], U32, name="v2_codes%d" % a, align_bytes=64) for a in range(R_PASSES)]
        v2_plane = keep.tile([P, S2], U8, align_bytes=64)
        nc.vector.tensor_copy(v2_codes[0][:], tab2_sb[0][:].bitcast(U32).indirect(bottles[:]))
        quantise_wa(0, wa_first, nc.vector.tensor_copy)
        waves = {0: cosine(0)}
        nc.vector.tensor_copy(v2_plane[:], tab2_plane[:].indirect(bottles[:]))
        nc.vector.tensor_copy(v2_codes[1][:], tab2_sb[1][:].bitcast(U32).indirect(bottles[:]))
        waves[1] = cosine(1)
        wa_second = load_wa(1)
        stock_sb = placed([P, M_TILES], F32, "stock_sb", AT_WA_RAW)
        with nc.allow_non_contiguous_dma(reason="one stock value a partition"):
            nc.sync.dma_start(stock_sb[:], stock.rearrange("(m p) -> p m", p=P))

        picked = [
            [keep.tile([P, PACK, MENUS], BF16, name="picked%d%d" % (c, a)) for a in range(R_PASSES)]
            for c in range(2)
        ]
        x_woven = [
            [keep.tile([P, PACK * MENUS], BF16, name="x_woven%d%d" % (c, a), align_bytes=64) for a in range(R_PASSES)]
            for c in range(2)
        ]
        x_codes, x_plane = {}, {}

        def pick(i):
            a, t = divmod(i, PACK)
            for_mains = work.tile([P, MENUS], F32, name="for_mains")
            nc.vector.tensor_copy(for_mains[:], hs[i][:].indirect(mains[:]))
            nc.vector.tensor_copy(picked[0][a][:, t, :], hs[i][:].indirect(starters[:]))
            nc.scalar.activation(picked[1][a][:, t, :], for_mains[:], ACT.Copy, scale=main_sb[:, a, t : t + 1])

        def weave(copy, c, a, first, last):
            copy(
                x_woven[c][a][:, PACK * first : PACK * last].rearrange("p (n i t) -> p n t i", i=4, t=PACK),
                picked[c][a][:, :, first:last].rearrange("p t (n i) -> p n t i", i=4),
            )

        def quantise_x(c, a):
            x_codes[c, a] = keep.tile([P, MENUS], U32, name="x_codes%d%d" % (c, a), align_bytes=64)
            x_plane[c, a] = keep.tile([P, MENUS], U8, name="x_plane%d%d" % (c, a), align_bytes=64)
            nc.vector.quantize_mx(out=x_codes[c, a][:].bitcast(FP8X4), scales=x_plane[c, a][:], in_=x_woven[c][a][:])

        def second_stage(acc, m, c, a, start, stop):
            cols = slice(m * P, (m + 1) * P)
            nc.tensor.matmul_mx(
                out=acc[:], lhsT=v2_codes[a][:, cols].bitcast(FP8X4), lhsT_scale=v2_plane[4 * a : P, cols],
                rhs=x_codes[c, a][:].bitcast(FP8X4), rhs_scale=x_plane[c, a][:],
                start=start, stop=stop,
            )

        def score_banks(m):
            return [bank((m + 1) % BANK_PAIRS, c) for c in range(2)]

        early = {}
        hs = {0: features(0)}
        for i in range(R_TILES):
            if i == 0:
                quantise_wa(1, wa_second, nc.scalar.copy)
            if i + 2 < R_TILES:
                waves[i + 2] = cosine(i + 2)
            if i + 1 < R_TILES:
                hs[i + 1] = features(i + 1)
            if i == R_TILES - 1:
                for c in range(2):
                    quantise_x(c, 0)
                    for m in range(EARLY_M_TILES):
                        if c == 0:
                            early[m] = score_banks(m)
                        second_stage(early[m][c], m, c, 0, True, False)
            pick(i)
            if PACK - 1 <= i < R_TILES - 1:
                c, part = divmod(i - PACK + 1, 2)
                weave(nc.scalar.copy, c, 0, part * MENUS // 2, (part + 1) * MENUS // 2)

        weave(nc.vector.tensor_copy, 0, 1, 0, MENUS)
        weave(nc.scalar.copy, 1, 1, 0, MENUS)
        quantise_x(0, 1)
        quantise_x(1, 1)

        for m in range(M_TILES):
            if m < EARLY_M_TILES:
                scores = early[m]
                for c in range(2):
                    second_stage(scores[c], m, c, 1, False, True)
            else:
                scores = score_banks(m)
                for c in range(2):
                    second_stage(scores[c], m, c, 1, True, False)
                    second_stage(scores[c], m, c, 0, False, True)
            starter_score = work.tile([P, MENUS], F32, name="starter_score", bufs=3)
            nc.scalar.copy(starter_score[:], scores[0][:])
            larger = work.tile([P, MENUS], F32, name="larger", bufs=3)
            nc.vector.tensor_tensor(larger[:], scores[1][:], starter_score[:], ALU.max)
            result = work.tile([P, MENUS], F32, name="result", bufs=4)
            factor = stock_sb[:, m : m + 1]
            if m == M_TILES - 1:
                nc.vector.tensor_scalar(result[:], larger[:], factor, None, ALU.mult)
            elif m % 2 == 0:
                nc.gpsimd.tensor_scalar(result[:], larger[:], factor, 0.0, ALU.mult, ALU.add)
            else:
                nc.scalar.activation(result[:], larger[:], ACT.Copy, scale=factor)
            nc.sync.dma_start(out[m * P : (m + 1) * P, :], result[:])
